import numpy as np
import ml_dtypes


def mxq(x, axis, fmt="e4m3"):
    dtype, down = {"e4m3": (ml_dtypes.float8_e4m3fn, 7), "e5m2": (ml_dtypes.float8_e5m2, 14)}[fmt]
    v = np.moveaxis(np.asarray(x, np.float32).astype(ml_dtypes.bfloat16).astype(np.float64), axis, -1)
    blocks = v.reshape(v.shape[:-1] + (-1, 32))
    amax = np.abs(blocks).max(-1, keepdims=True)
    byte = np.maximum(np.where(amax > 0, np.frexp(amax)[1] - 1 + 127, 0) - down, 1)
    scale = np.exp2(byte - 127.0)
    codes = (blocks / scale).astype(np.float32).astype(dtype).astype(np.float64)
    return np.moveaxis((codes * scale).reshape(v.shape), -1, axis)


WIDE = False


def mx_kscale(k):
    if not WIDE:
        return np.ones(k)
    levels = np.array([10, -10, 5, -5, 0])
    if k % 512:
        return np.exp2(np.random.permutation(np.resize(levels, k // 32))).repeat(32)
    a = np.empty((k // 512, 16))
    for p in range(k // 512):
        a[p, :8] = np.random.permutation(np.resize(levels, 8))
        for g in range(8):
            far = levels[np.abs(levels - a[p, g]) >= 10]
            a[p, g + 8] = far[np.random.randint(len(far))]
    return np.exp2(a.ravel()).repeat(32)


def f64(x):
    return np.asarray(x).astype(np.float64)


def striped8(idx):
    return np.asarray(idx).reshape(8, -1, 16).transpose(0, 2, 1).reshape(128, -1).astype(np.uint16)


def unstriped8(offs):
    return offs.reshape(8, 16, -1).transpose(0, 2, 1).reshape(8, -1).astype(np.int64)


def pick8(x, idx, run):
    r = np.arange(len(x))
    return x[r[:, None], idx[r % (8 * run) // run]]


E2M1 = np.array([0.0, 0.5, 1.0, 1.5, 2.0, 3.0, 4.0, 6.0, -0.0, -0.5, -1.0, -1.5, -2.0, -3.0, -4.0, -6.0])


def pack_weight(w, fmt):
    k, n = w.shape
    w = f64(np.asarray(w, np.float32).astype(ml_dtypes.bfloat16)).reshape(k // 32, 32, n)
    amax = np.abs(w).max(1)
    if fmt == "e4m3":
        byte = np.frexp(amax)[1] - 1 + 127 - 7
    else:
        mant, ex = np.frexp(amax / 6.0)
        byte = np.where(mant > 0.5, ex, ex - 1) + 127
    byte = np.clip(np.where(amax > 0, byte, 1), 1, 254)
    scaled = (w * np.exp2(127.0 - byte)[:, None, :]).reshape(k, n).astype(np.float32)
    by_word = np.ascontiguousarray(scaled.reshape(k // 512, 128, 4, n).transpose(0, 1, 3, 2))
    if fmt == "e4m3":
        words = by_word.astype(ml_dtypes.float8_e4m3fn).view(np.uint8)
    else:
        c = by_word.astype(ml_dtypes.float4_e2m1fn).view(np.uint8) & 0xF
        words = (c[..., 0::2] | (c[..., 1::2] << 4)).reshape(k // 512, 128, 2 * n)
    return np.ascontiguousarray(words), np.ascontiguousarray(byte.astype(np.uint8).reshape(k // 512, 16, n))


def unpack_weight(words, scales, fmt):
    g, _, n = scales.shape
    words = np.ascontiguousarray(words).reshape(g, 128, n, -1)
    if fmt == "e4m3":
        vals = words.view(ml_dtypes.float8_e4m3fn).astype(np.float64)
    else:
        nib = np.empty((g, 128, n, 4), np.uint8)
        nib[..., 0::2] = words & 0xF
        nib[..., 1::2] = words >> 4
        vals = E2M1[nib]
    vals = vals * np.repeat(np.exp2(scales.astype(np.float64) - 127.0), 8, axis=1)[..., None]
    return vals.transpose(0, 1, 3, 2).reshape(g * 512, n)


D, T, U, I, Q = 512, 1024, 1024, 512, 128


def setup_inputs():
    n = np.random.standard_normal
    idx = np.stack([np.random.permutation(T)[:I] for _ in range(8)])
    idx2 = np.stack([np.random.permutation(U)[:I] for _ in range(8)])
    idx3 = np.stack([np.random.permutation(U)[:I] for _ in range(8)])
    fd = mx_kscale(D)
    keysp = pack_weight(n((D, T)) / fd[:, None], "e4m3")
    notesp = pack_weight(n((D, U)) / fd[:, None], "e2m1")
    return {
        "query": (n((D, Q)) * 1.0 / np.sqrt(D) * fd[:, None]).astype(np.float32),
        "keys_words": keysp[0],
        "keys_scales": keysp[1],
        "notes_words": notesp[0],
        "notes_scales": notesp[1],
        "offs": striped8(idx),
        "offs2": striped8(idx2),
        "offs3": striped8(idx3),
    }


def reference(query, keys_words, keys_scales, notes_words, notes_scales, offs, offs2, offs3):
    idx = unstriped8(offs)
    idx2 = unstriped8(offs2)
    idx3 = unstriped8(offs3)
    keysu = unpack_weight(keys_words, keys_scales, "e4m3")
    notesu = unpack_weight(notes_words, notes_scales, "e2m1")
    queryq = mxq(f64(query), 0, "e4m3")
    a = queryq.T @ keysu
    b = queryq.T @ notesu
    ta = np.max(a, axis=1, keepdims=True)
    e1 = np.exp(pick8(a, idx, 16) - ta)
    f1 = np.zeros((Q, U))
    f1[np.arange(Q)[:, None], idx2[np.arange(Q) % 128 // 16]] = e1
    m2 = np.maximum(f1 * 8.0, b)
    y = pick8(m2, idx3, 16) - e1
    return y

@@ -1,0 +1,141 @@
+from contextlib import ExitStack
+
+import concourse.mybir as mybir
+
+D, T, U, SLOTS, Q = 512, 1024, 1024, 512, 128
+FLOPS = 2 * Q * D * (T + U)
+
+F32 = mybir.dt.float32
+BF16 = mybir.dt.bfloat16
+I32 = mybir.dt.int32
+U32 = mybir.dt.uint32
+U16 = mybir.dt.uint16
+U8 = mybir.dt.uint8
+FP8X4 = mybir.dt.float8_e4m3fn_x4
+FP4X4 = mybir.dt.float4_e2m1fn_x4
+ALU = mybir.AluOpType
+ACT = mybir.ActivationFunctionType
+
+P = 128
+PACK = 4
+KEY_LOAD = 512
+KEY_PASS = 256
+NOTE_PASS = 512
+HALF = SLOTS // 2
+
+
+def load_scale_rows(nc, plane, scales):
+    for quad in range(4):
+        nc.sync.dma_start(
+            out=plane[32 * quad : 32 * quad + 4, :].bitcast(I32),
+            in_=scales[0, 4 * quad : 4 * quad + 4, :].bitcast(I32),
+        )
+
+
+def tile_attend_larger_two_kernel(
+    tc, query, keys_words, keys_scales, notes_words, notes_scales, offs, offs2, offs3, out
+):
+    nc = tc.nc
+    with ExitStack() as ctx:
+        sb = ctx.enter_context(tc.tile_pool(name="sb", bufs=1))
+        psum = ctx.enter_context(tc.psum_pool(name="psum", bufs=1))
+
+        key_plane = sb.tile([P, T], U8, name="key_plane", align_bytes=64)
+        nc.vector.memset(key_plane[:].bitcast(I32), 0)
+
+        q_raw = sb.tile([P, PACK, Q], F32, name="q_raw")
+        nc.sync.dma_start(out=q_raw[:], in_=query.rearrange("(p t) q -> p t q", t=PACK))
+
+        key_rows = keys_words[0].rearrange("p n t -> p (n t)").bitcast(I32)
+        key_words = []
+        for h in range(T // KEY_LOAD):
+            words = sb.tile([P, KEY_LOAD], U32, name="key_words%d" % h, align_bytes=64)
+            nc.sync.dma_start(out=words[:].bitcast(I32), in_=key_rows[:, h * KEY_LOAD : (h + 1) * KEY_LOAD])
+            key_words.append(words)
+        load_scale_rows(nc, key_plane, keys_scales)
+
+        token_list = sb.tile([P, SLOTS // 16], U16, name="token_list")
+        nc.sync.dma_start(token_list[:], offs)
+        put_list = sb.tile([P, SLOTS // 16], U16, name="put_list")
+        nc.sync.dma_start(put_list[:], offs2)
+
+        f1 = sb.tile([P, U], F32, name="f1")
+        nc.vector.memset(f1[:], 0.0)
+        note_plane = sb.tile([P, U], U8, name="note_plane", align_bytes=64)
+        nc.vector.memset(note_plane[:].bitcast(I32), 0)
+
+        note_words = sb.tile([P, 2 * U], U8, name="note_words", align_bytes=64)
+        nc.sync.dma_start(out=note_words[:].bitcast(I32), in_=notes_words[0].bitcast(I32))
+        load_scale_rows(nc, note_plane, notes_scales)
+        read_list = sb.tile([P, SLOTS // 16], U16, name="read_list")
+        nc.sync.dma_start(read_list[:], offs3)
+
+        q_bf16 = sb.tile([P, Q, PACK], BF16, name="q_bf16", align_bytes=64)
+        nc.vector.tensor_copy(out=q_bf16[:], in_=q_raw[:].rearrange("p t q -> p q t"))
+        q_words = sb.tile([P, Q], U32, name="q_words", align_bytes=64)
+        q_plane = sb.tile([P, Q], U8, name="q_plane", align_bytes=64)
+        nc.vector.quantize_mx(
+            out=q_words[:].bitcast(FP8X4), scales=q_plane[:], in_=q_bf16[:].rearrange("p q t -> p (q t)")
+        )
+
+        a = sb.tile([P, T], F32, name="a")
+        part_max = sb.tile([P, T // KEY_PASS], F32, name="part_max")
+        for j in range(T // KEY_PASS):
+            h, c0 = divmod(j * KEY_PASS, KEY_LOAD)
+            cols = slice(j * KEY_PASS, (j + 1) * KEY_PASS)
+            bank = psum.tile([P, KEY_PASS], F32, name="a_bank%d" % j)
+            nc.tensor.matmul_mx(
+                out=bank[:],
+                lhsT=q_words[:].bitcast(FP8X4),
+                lhsT_scale=q_plane[:],
+                rhs=key_words[h][:, c0 : c0 + KEY_PASS].bitcast(FP8X4),
+                rhs_scale=key_plane[:, cols],
+                start=True,
+                stop=True,
+            )
+            nc.vector.tensor_scalar(
+                out=a[:, cols],
+                in0=bank[:],
+                scalar1=1.0,
+                scalar2=None,
+                op0=ALU.mult,
+                op1=ALU.max,
+                accum_out=part_max[:, j : j + 1],
+            )
+        neg_ta = sb.tile([P, 1], F32, name="neg_ta")
+        nc.vector.tensor_reduce(out=neg_ta[:], in_=part_max[:], axis=mybir.AxisListType.X, op=ALU.max, negate=True)
+
+        b_banks = []
+        for j in range(U // NOTE_PASS):
+            bank = psum.tile([P, NOTE_PASS], F32, name="b_bank%d" % j)
+            nc.tensor.matmul_mx(
+                out=bank[:],
+                lhsT=q_words[:].bitcast(FP8X4),
+                lhsT_scale=q_plane[:],
+                rhs=note_words[:, 2 * j * NOTE_PASS : 2 * (j + 1) * NOTE_PASS].bitcast(FP4X4),
+                rhs_scale=note_plane[:, j * NOTE_PASS : (j + 1) * NOTE_PASS],
+                start=True,
+                stop=True,
+            )
+            b_banks.append(bank)
+
+        halves = [slice(h * HALF // 16, (h + 1) * HALF // 16) for h in range(2)]
+        e1 = [sb.tile([P, HALF], F32, name="e1_%d" % h) for h in range(2)]
+        for h in range(2):
+            nc.scalar.activation(e1[h][:], a[:].indirect(token_list[:, halves[h]]), ACT.Exp, bias=neg_ta[:])
+            nc.vector.tensor_copy(f1[:].indirect(put_list[:, halves[h]]), e1[h][:])
+
+        m2 = sb.tile([P, U], F32, name="m2")
+        for j in range(U // NOTE_PASS):
+            cols = slice(j * NOTE_PASS, (j + 1) * NOTE_PASS)
+            nc.vector.scalar_tensor_tensor(
+                out=m2[:, cols], in0=f1[:, cols], scalar=8.0, in1=b_banks[j][:], op0=ALU.mult, op1=ALU.max
+            )
+
+        y = [sb.tile([P, HALF], F32, name="y_%d" % h) for h in range(2)]
+        picked = sb.tile([P, HALF], F32, name="picked")
+        nc.scalar.activation(picked[:], m2[:].indirect(read_list[:, halves[1]]), ACT.Copy)
+        nc.vector.tensor_tensor(y[0][:], m2[:].indirect(read_list[:, halves[0]]), e1[0][:], ALU.subtract)
+        nc.sync.dma_start(out=out[:, 0:HALF], in_=y[0][:])
+        nc.vector.tensor_tensor(y[1][:], picked[:], e1[1][:], ALU.subtract)
+        nc.scalar.dma_start(out=out[:, HALF:SLOTS], in_=y[1][:])

@@ -41,18 +41,17 @@ def tile_attend_larger_two_kernel(
         psum = ctx.enter_context(tc.psum_pool(name="psum", bufs=1))
 
         key_plane = sb.tile([P, T], U8, name="key_plane", align_bytes=64)
-        nc.vector.memset(key_plane[:].bitcast(I32), 0)
 
         q_raw = sb.tile([P, PACK, Q], F32, name="q_raw")
         nc.sync.dma_start(out=q_raw[:], in_=query.rearrange("(p t) q -> p t q", t=PACK))
 
+        load_scale_rows(nc, key_plane, keys_scales)
         key_rows = keys_words[0].rearrange("p n t -> p (n t)").bitcast(I32)
         key_words = []
         for h in range(T // KEY_LOAD):
             words = sb.tile([P, KEY_LOAD], U32, name="key_words%d" % h, align_bytes=64)
             nc.sync.dma_start(out=words[:].bitcast(I32), in_=key_rows[:, h * KEY_LOAD : (h + 1) * KEY_LOAD])
             key_words.append(words)
-        load_scale_rows(nc, key_plane, keys_scales)
 
         token_list = sb.tile([P, SLOTS // 16], U16, name="token_list")
         nc.sync.dma_start(token_list[:], offs)
@@ -62,7 +61,6 @@ def tile_attend_larger_two_kernel(
         f1 = sb.tile([P, U], F32, name="f1")
         nc.vector.memset(f1[:], 0.0)
         note_plane = sb.tile([P, U], U8, name="note_plane", align_bytes=64)
-        nc.vector.memset(note_plane[:].bitcast(I32), 0)
 
         note_words = sb.tile([P, 2 * U], U8, name="note_words", align_bytes=64)
         nc.sync.dma_start(out=note_words[:].bitcast(I32), in_=notes_words[0].bitcast(I32))
@@ -71,7 +69,9 @@ def tile_attend_larger_two_kernel(
         nc.sync.dma_start(read_list[:], offs3)
 
         q_bf16 = sb.tile([P, Q, PACK], BF16, name="q_bf16", align_bytes=64)
-        nc.vector.tensor_copy(out=q_bf16[:], in_=q_raw[:].rearrange("p t q -> p q t"))
+        q_turned = q_raw[:].rearrange("p t q -> p q t")
+        nc.vector.tensor_copy(out=q_bf16[:, 0:80, :], in_=q_turned[:, 0:80, :])
+        nc.scalar.activation(q_bf16[:, 80:Q, :], q_turned[:, 80:Q, :], ACT.Copy)
         q_words = sb.tile([P, Q], U32, name="q_words", align_bytes=64)
         q_plane = sb.tile([P, Q], U8, name="q_plane", align_bytes=64)
         nc.vector.quantize_mx(
@@ -138,4 +138,4 @@ def tile_attend_larger_two_kernel(
         nc.vector.tensor_tensor(y[0][:], m2[:].indirect(read_list[:, halves[0]]), e1[0][:], ALU.subtract)
         nc.sync.dma_start(out=out[:, 0:HALF], in_=y[0][:])
         nc.vector.tensor_tensor(y[1][:], picked[:], e1[1][:], ALU.subtract)
-        nc.scalar.dma_start(out=out[:, HALF:SLOTS], in_=y[1][:])
+        nc.sync.dma_start(out=out[:, HALF:SLOTS], in_=y[1][:])

@@ -133,9 +133,6 @@ def tile_attend_larger_two_kernel(
             )
 
         y = [sb.tile([P, HALF], F32, name="y_%d" % h) for h in range(2)]
-        picked = sb.tile([P, HALF], F32, name="picked")
-        nc.scalar.activation(picked[:], m2[:].indirect(read_list[:, halves[1]]), ACT.Copy)
-        nc.vector.tensor_tensor(y[0][:], m2[:].indirect(read_list[:, halves[0]]), e1[0][:], ALU.subtract)
-        nc.sync.dma_start(out=out[:, 0:HALF], in_=y[0][:])
-        nc.vector.tensor_tensor(y[1][:], picked[:], e1[1][:], ALU.subtract)
-        nc.sync.dma_start(out=out[:, HALF:SLOTS], in_=y[1][:])
+        for h in range(2):
+            nc.vector.tensor_tensor(y[h][:], m2[:].indirect(read_list[:, halves[h]]), e1[h][:], ALU.subtract)
+            nc.sync.dma_start(out=out[:, h * HALF : (h + 1) * HALF], in_=y[h][:])

@@ -69,9 +69,10 @@ def tile_attend_larger_two_kernel(
         nc.sync.dma_start(read_list[:], offs3)
 
         q_bf16 = sb.tile([P, Q, PACK], BF16, name="q_bf16", align_bytes=64)
-        q_turned = q_raw[:].rearrange("p t q -> p q t")
-        nc.vector.tensor_copy(out=q_bf16[:, 0:80, :], in_=q_turned[:, 0:80, :])
-        nc.scalar.activation(q_bf16[:, 80:Q, :], q_turned[:, 80:Q, :], ACT.Copy)
+        q_src = q_raw[:].rearrange("p t (c i) -> p c t i", i=4)
+        q_dst = q_bf16[:].rearrange("p (c i) t -> p c t i", i=4)
+        nc.vector.tensor_copy(out=q_dst[:, 0:20], in_=q_src[:, 0:20])
+        nc.scalar.activation(q_dst[:, 20:32], q_src[:, 20:32], ACT.Copy)
         q_words = sb.tile([P, Q], U32, name="q_words", align_bytes=64)
         q_plane = sb.tile([P, Q], U8, name="q_plane", align_bytes=64)
         nc.vector.quantize_mx(

from contextlib import ExitStack

import concourse.mybir as mybir

D, T, U, SLOTS, Q = 512, 1024, 1024, 512, 128
FLOPS = 2 * Q * D * (T + U)

F32 = mybir.dt.float32
BF16 = mybir.dt.bfloat16
I32 = mybir.dt.int32
U32 = mybir.dt.uint32
U16 = mybir.dt.uint16
U8 = mybir.dt.uint8
FP8X4 = mybir.dt.float8_e4m3fn_x4
FP4X4 = mybir.dt.float4_e2m1fn_x4
ALU = mybir.AluOpType
ACT = mybir.ActivationFunctionType

P = 128
PACK = 4
KEY_LOAD = 512
KEY_PASS = 256
NOTE_PASS = 512
HALF = SLOTS // 2


def load_scale_rows(nc, plane, scales):
    for quad in range(4):
        nc.sync.dma_start(
            out=plane[32 * quad : 32 * quad + 4, :].bitcast(I32),
            in_=scales[0, 4 * quad : 4 * quad + 4, :].bitcast(I32),
        )


def tile_attend_larger_two_kernel(
    tc, query, keys_words, keys_scales, notes_words, notes_scales, offs, offs2, offs3, out
):
    nc = tc.nc
    with ExitStack() as ctx:
        sb = ctx.enter_context(tc.tile_pool(name="sb", bufs=1))
        psum = ctx.enter_context(tc.psum_pool(name="psum", bufs=1))

        key_plane = sb.tile([P, T], U8, name="key_plane", align_bytes=64)

        q_raw = sb.tile([P, PACK, Q], F32, name="q_raw")
        nc.sync.dma_start(out=q_raw[:], in_=query.rearrange("(p t) q -> p t q", t=PACK))

        load_scale_rows(nc, key_plane, keys_scales)
        key_rows = keys_words[0].rearrange("p n t -> p (n t)").bitcast(I32)
        key_words = []
        for h in range(T // KEY_LOAD):
            words = sb.tile([P, KEY_LOAD], U32, name="key_words%d" % h, align_bytes=64)
            nc.sync.dma_start(out=words[:].bitcast(I32), in_=key_rows[:, h * KEY_LOAD : (h + 1) * KEY_LOAD])
            key_words.append(words)

        token_list = sb.tile([P, SLOTS // 16], U16, name="token_list")
        nc.sync.dma_start(token_list[:], offs)
        put_list = sb.tile([P, SLOTS // 16], U16, name="put_list")
        nc.sync.dma_start(put_list[:], offs2)

        f1 = sb.tile([P, U], F32, name="f1")
        nc.vector.memset(f1[:], 0.0)
        note_plane = sb.tile([P, U], U8, name="note_plane", align_bytes=64)

        note_words = sb.tile([P, 2 * U], U8, name="note_words", align_bytes=64)
        nc.sync.dma_start(out=note_words[:].bitcast(I32), in_=notes_words[0].bitcast(I32))
        load_scale_rows(nc, note_plane, notes_scales)
        read_list = sb.tile([P, SLOTS // 16], U16, name="read_list")
        nc.sync.dma_start(read_list[:], offs3)

        q_bf16 = sb.tile([P, Q, PACK], BF16, name="q_bf16", align_bytes=64)
        q_src = q_raw[:].rearrange("p t (c i) -> p c t i", i=4)
        q_dst = q_bf16[:].rearrange("p (c i) t -> p c t i", i=4)
        nc.vector.tensor_copy(out=q_dst[:, 0:20], in_=q_src[:, 0:20])
        nc.scalar.activation(q_dst[:, 20:32], q_src[:, 20:32], ACT.Copy)
        q_words = sb.tile([P, Q], U32, name="q_words", align_bytes=64)
        q_plane = sb.tile([P, Q], U8, name="q_plane", align_bytes=64)
        nc.vector.quantize_mx(
            out=q_words[:].bitcast(FP8X4), scales=q_plane[:], in_=q_bf16[:].rearrange("p q t -> p (q t)")
        )

        a = sb.tile([P, T], F32, name="a")
        part_max = sb.tile([P, T // KEY_PASS], F32, name="part_max")
        for j in range(T // KEY_PASS):
            h, c0 = divmod(j * KEY_PASS, KEY_LOAD)
            cols = slice(j * KEY_PASS, (j + 1) * KEY_PASS)
            bank = psum.tile([P, KEY_PASS], F32, name="a_bank%d" % j)
            nc.tensor.matmul_mx(
                out=bank[:],
                lhsT=q_words[:].bitcast(FP8X4),
                lhsT_scale=q_plane[:],
                rhs=key_words[h][:, c0 : c0 + KEY_PASS].bitcast(FP8X4),
                rhs_scale=key_plane[:, cols],
                start=True,
                stop=True,
            )
            nc.vector.tensor_scalar(
                out=a[:, cols],
                in0=bank[:],
                scalar1=1.0,
                scalar2=None,
                op0=ALU.mult,
                op1=ALU.max,
                accum_out=part_max[:, j : j + 1],
            )
        neg_ta = sb.tile([P, 1], F32, name="neg_ta")
        nc.vector.tensor_reduce(out=neg_ta[:], in_=part_max[:], axis=mybir.AxisListType.X, op=ALU.max, negate=True)

        b_banks = []
        for j in range(U // NOTE_PASS):
            bank = psum.tile([P, NOTE_PASS], F32, name="b_bank%d" % j)
            nc.tensor.matmul_mx(
                out=bank[:],
                lhsT=q_words[:].bitcast(FP8X4),
                lhsT_scale=q_plane[:],
                rhs=note_words[:, 2 * j * NOTE_PASS : 2 * (j + 1) * NOTE_PASS].bitcast(FP4X4),
                rhs_scale=note_plane[:, j * NOTE_PASS : (j + 1) * NOTE_PASS],
                start=True,
                stop=True,
            )
            b_banks.append(bank)

        halves = [slice(h * HALF // 16, (h + 1) * HALF // 16) for h in range(2)]
        e1 = [sb.tile([P, HALF], F32, name="e1_%d" % h) for h in range(2)]
        for h in range(2):
            nc.scalar.activation(e1[h][:], a[:].indirect(token_list[:, halves[h]]), ACT.Exp, bias=neg_ta[:])
            nc.vector.tensor_copy(f1[:].indirect(put_list[:, halves[h]]), e1[h][:])

        m2 = sb.tile([P, U], F32, name="m2")
        for j in range(U // NOTE_PASS):
            cols = slice(j * NOTE_PASS, (j + 1) * NOTE_PASS)
            nc.vector.scalar_tensor_tensor(
                out=m2[:, cols], in0=f1[:, cols], scalar=8.0, in1=b_banks[j][:], op0=ALU.mult, op1=ALU.max
            )

        y = [sb.tile([P, HALF], F32, name="y_%d" % h) for h in range(2)]
        for h in range(2):
            nc.vector.tensor_tensor(y[h][:], m2[:].indirect(read_list[:, halves[h]]), e1[h][:], ALU.subtract)
            nc.sync.dma_start(out=out[:, h * HALF : (h + 1) * HALF], in_=y[h][:])
